import numpy as np
import ml_dtypes


def mxq(x, axis, fmt="e4m3"):
    dtype, down = {"e4m3": (ml_dtypes.float8_e4m3fn, 7), "e5m2": (ml_dtypes.float8_e5m2, 14)}[fmt]
    v = np.moveaxis(np.asarray(x, np.float32).astype(ml_dtypes.bfloat16).astype(np.float64), axis, -1)
    blocks = v.reshape(v.shape[:-1] + (-1, 32))
    amax = np.abs(blocks).max(-1, keepdims=True)
    byte = np.maximum(np.where(amax > 0, np.frexp(amax)[1] - 1 + 127, 0) - down, 1)
    scale = np.exp2(byte - 127.0)
    codes = (blocks / scale).astype(np.float32).astype(dtype).astype(np.float64)
    return np.moveaxis((codes * scale).reshape(v.shape), -1, axis)


WIDE = False


def mx_kscale(k):
    if not WIDE:
        return np.ones(k)
    levels = np.array([10, -10, 5, -5, 0])
    if k % 512:
        return np.exp2(np.random.permutation(np.resize(levels, k // 32))).repeat(32)
    a = np.empty((k // 512, 16))
    for p in range(k // 512):
        a[p, :8] = np.random.permutation(np.resize(levels, 8))
        for g in range(8):
            far = levels[np.abs(levels - a[p, g]) >= 10]
            a[p, g + 8] = far[np.random.randint(len(far))]
    return np.exp2(a.ravel()).repeat(32)


BF16 = ml_dtypes.bfloat16


def bf(x):
    return np.asarray(x, np.float32).astype(BF16)


def f64(x):
    return np.asarray(x).astype(np.float64)

def planes(Y):
    n, m = Y.shape
    b = f64(bf(Y)).reshape(n // 32, 32, m)
    amax = np.abs(b).max(1)
    byte = np.clip(np.where(amax > 0, np.frexp(amax)[1] - 1 + 127 - 7, 1), 1, 254)
    codes = (b * np.exp2(127.0 - byte)[:, None, :]).reshape(n, m).astype(np.float32).astype(ml_dtypes.float8_e4m3fn).view(np.uint8)
    words = codes.reshape(n // 512, 128, 4, m).transpose(0, 1, 3, 2)
    return np.ascontiguousarray(words), np.ascontiguousarray(byte.astype(np.uint8).reshape(n // 512, 16, m))


M, D, J, N = 2048, 512, 1024, 1024


def setup_inputs():
    s = mx_kscale(D)
    t = mx_kscale(J)
    x = np.random.randn(M, D) * s
    z = 0.7 * np.random.randn(J, D) / np.sqrt(D) / s
    amp = np.exp(0.3 * np.random.randn(J)) * t
    w = np.random.randn(J, N) / np.sqrt(J) / t[:, None]
    mean = 0.8 * np.random.randn(M, N)
    state_scale = np.exp(0.8 * np.random.randn(N))
    return {"x": bf(x), "z": bf(z), "amp": bf(amp), "w": bf(w),
            "mean": bf(mean), "state_scale": bf(state_scale)}


def reference(x, z, amp, w, mean, state_scale):
    x, z, amp, w = f64(x), f64(z), f64(amp), f64(w)
    mean, state_scale = f64(mean), f64(state_scale)
    dots = mxq(z, 1, "e4m3") @ mxq(x, 1, "e4m3").T
    kzx = np.exp(dots) * amp[:, None]
    f = mxq(kzx, 0, "e4m3").T @ mxq(w, 0, "e4m3")
    y = (f + mean) * state_scale
    Y = y.T
    words, scales = planes(Y)
    return y, words, scales

@@ -1,0 +1,388 @@
+import math
+from contextlib import ExitStack
+
+import concourse.mybir as mybir
+from concourse.masks import make_identity
+
+M, D, J, N = 2048, 512, 1024, 1024
+FLOPS = 2 * J * M * D + 2 * M * J * N
+P = 128
+F32 = mybir.dt.float32
+BF16 = mybir.dt.bfloat16
+I32 = mybir.dt.int32
+U32 = mybir.dt.uint32
+U8 = mybir.dt.uint8
+FP8X4 = mybir.dt.float8_e4m3fn_x4
+ALU = mybir.AluOpType
+ACT = mybir.ActivationFunctionType
+
+BUFS = dict(sbank=4, s2bank=3, kzi=1, kzv=3, ez=3, y=4, tmp=2, yc=2, yi=2, wsg=4, wil=2, xi=2, zi=2)
+FOUR = False
+GM = {9: 256, 10: 320, 11: 320, 12: 320, 13: 448, 14: 448}
+GC = dict((s, 80) for s in range(1, 9))
+GK = {9: 128, 10: 128, 11: 128, 12: 128}
+
+
+def schedule(P):
+    ops = []
+
+    def add(*op):
+        ops.append(op)
+
+    for l in P["loads"]:
+        add("load", *l)
+    add("consts")
+    add("amp_pre")
+    add("ln")
+    add("amp_post")
+    for op in P["head"]:
+        add(*op)
+    S = 16
+    for s in range(S):
+        for op in P["g"].get(s, []):
+            add(*op)
+        add("ad", s, 0)
+        add("ad", s, 1)
+        if s in GC:
+            add("ca", s - 1, 0, GC[s], "G")
+        if s in GM:
+            add("mu", s, 0, GM[s], "G")
+            add("mu", s, GM[s], 512, "V")
+        else:
+            add("mu", s, 0, 512, "V")
+        if s == S - 1:
+            add("sty", s, 0)
+        add("mu", s, 512, 1024, "V")
+        if s == S - 1:
+            add("sty", s, 1)
+        else:
+            add("sty", s)
+        if s >= 1:
+            add("ca", s - 1, GC.get(s, 0), 256, "S")
+        if s >= 2:
+            add("yt", s - 2)
+        for op in P["xt"].get(s, []):
+            add(*op)
+        if s >= 2:
+            add("yw", s - 2)
+        for op in P["xc"].get(s, []):
+            add(*op)
+        if s + 1 < S:
+            add("s2", s + 1, 0)
+            add("s2", s + 1, 1)
+        for op in P["ex"].get(s, []):
+            add("s1", *op)
+            add("ex", *op)
+        for op in P["sk"].get(s, []):
+            add(*op)
+        if s >= 2:
+            add("yq", s - 2, 0)
+            add("yq", s - 2, 1)
+            if (s - 2) % 4 == 3:
+                add("stw", s - 5, s - 1)
+            if s - 2 == 11:
+                add("sts", 0, 12)
+        for op in P["vq"].get(s, []):
+            add(*op)
+    add("yt", 14)
+    add("ca", 15, 0, 128, "S")
+    add("yw", 14)
+    add("ca", 15, 128, 256, "V")
+    add("yt", 15, 0)
+    add("yt", 15, 1)
+    add("yq", 14, 0)
+    add("yq", 14, 1)
+    add("stw", 12, 15)
+    add("yw", 15, 0)
+    add("yw", 15, 1)
+    add("yq", 15, 0)
+    add("yq", 15, 1)
+    add("stw", 15, 16)
+    add("sts", 12, 16)
+    return ops
+
+
+def params():
+    P = {}
+    P["loads"] = [("amp",), ("z", 0), ("w", 0, 0), ("x", 0), ("w", 1, 0), ("z", 1), ("ss",), ("w", 0, 1), ("w", 1, 1), ("x", 1), ("mean", 0), ("mean", 1), ("x", 2), ("mean", 2), ("mean", 3), ("x", 3)] + [("mean", i) for i in range(4, 8)]
+    H = []
+    H += [("zt", 0, 0), ("zt", 0, 1), ("zc", 0, 0), ("zc", 0, 1)]
+    H += [("ws", 0, 0), ("wi", 0, 0, "V"), ("zq", 0)]
+    H += [("xt", 0, 0), ("xt", 0, 1), ("xc", 0, 0), ("xc", 0, 1)]
+    H += [("ws", 1, 0), ("wi", 1, 0, "S"), ("wq", 0, 0), ("xq", 0)]
+    H += [("zt", 1, 0), ("zt", 1, 1)]
+    H += [("s1", 0, 0, 0), ("s1", 0, 0, 1), ("zc", 1, 0), ("zc", 1, 1), ("ex", 0, 0, 0), ("ex", 0, 0, 1)]
+    H += [("ws", 0, 1), ("wi", 0, 1, "V"), ("wq", 1, 0), ("zq", 1), ("ws", 1, 1), ("wq", 0, 1), ("wi", 1, 1, "V")]
+    for t in range(2, 4):
+        H += [("s1", 0, 0, t), ("ex", 0, 0, t)]
+    H += [("xt", 1, 0), ("xt", 1, 1), ("sst",), ("xc", 1, 0), ("xc", 1, 1)]
+    for t in range(4):
+        H += [("s1", 0, 1, t), ("ex", 0, 1, t)]
+    H += [("xq", 1), ("ki", 0, 0, 0, 0, 256, "V", "kzv"), ("wq", 1, 1), ("ki", 0, 0, 1, 0, 256, "V", "kzi"), ("kq", 0, 0, 0), ("ki", 0, 1, 0, 0, 256, "V", "kzv"), ("kq", 0, 1, 0), ("kq", 0, 0, 1)]
+    for t in range(3):
+        H += [("s1", 1, 0, t), ("ex", 1, 0, t)]
+    H += [("s2", 0, 0), ("s2", 0, 1), ("s1", 1, 0, 3), ("ex", 1, 0, 3)]
+    P["head"] = H
+    P["g"], P["vq"], P["ex"], P["xt"], P["xc"], P["sk"] = {}, {}, {}, {}, {}, {}
+    P["g"][0] = [("ki", 0, 1, 1, 0, 256, "G", "kzi")]
+    P["vq"][0] = [("kq", 0, 1, 1)]
+    for k in (1, 2, 3):
+        for n, (g, hf) in enumerate([(0, 0), (1, 0), (0, 1), (1, 1)]):
+            s = 4 * k - 3 + n
+            m1 = GK.get(s, 256)
+            P["g"].setdefault(s, []).append(("ki", k, g, hf, 0, m1, "G", "kzi"))
+            if m1 < 256:
+                P["g"][s].append(("ki", k, g, hf, m1, 256, "S", "kzi"))
+            P["vq"].setdefault(s, []).append(("kq", k, g, hf))
+    P["ex"][0] = [(1, 1, t) for t in range(4)]
+    for k in (2, 3):
+        s0 = 4 * k - 7
+        for n in range(4):
+            P["ex"].setdefault(s0 + n, []).extend([(k, n // 2, 2 * (n % 2)), (k, n // 2, 2 * (n % 2) + 1)])
+    P["xt"][0] = [("xt", 2, 0), ("xt", 2, 1)]
+    P["xc"][0] = [("xc", 2, 0), ("xc", 2, 1)]
+    P["vq"][0].insert(0, ("xq", 2))
+    P["sk"][7] = [("ssc",)]
+    for n in range(2):
+        P["xt"][3 + n] = [("xt", 3, n)]
+        P["xc"][3 + n] = [("xc", 3, n)]
+    P["vq"][4].insert(0, ("xq", 3))
+    return P
+
+
+def tile_inducing_kernel_mean_h3_kernel(tc, x, z, amp, w, mean, state_scale, out_0, out_1, out_2):
+    nc = tc.nc
+    with ExitStack() as ctx:
+        sb = ctx.enter_context(tc.tile_pool(name="sb", bufs=1))
+        ps = ctx.enter_context(tc.psum_pool(name="ps", bufs=1))
+        ctx.enter_context(tc.manual_schedule())
+        T = {}
+        count = {}
+
+        def rot(pool, tag, key, shape, dtype):
+            if key not in T:
+                n = count.get(tag, 0)
+                count[tag] = n + 1
+                name = "%s%d" % (tag, n % BUFS[tag])
+                if pool is ps:
+                    T[key] = pool.tile(shape, dtype, name=name, tag=name)
+                else:
+                    T[key] = pool.tile(shape, dtype, name=name, tag=name, align_bytes=64)
+            return T[key]
+
+        def keep(name, shape, dtype):
+            return sb.tile(shape, dtype, name=name, tag=name, align_bytes=64)
+
+        ident = keep("ident", [P, P], F32)
+        one = keep("one", [P, 1], F32)
+        warm = keep("warm", [P, 1], F32)
+        amp_bf = keep("amp_bf", [P, 8], BF16)
+        mant = keep("mant", [P, 4], I32)
+        amp32 = keep("amp32", [P, 8], F32)
+        exp_i = keep("exp_i", [P, 8], I32)
+        exp_f = keep("exp_f", [P, 8], F32)
+        sign2 = keep("sign2", [P, 8], F32)
+        sign = keep("sign", [P, 8], F32)
+        dead = keep("dead", [P, 8], F32)
+        ln_pow = keep("ln_pow", [P, 8], F32)
+        ln_part = keep("ln_part", [P, 8], F32)
+        ln_mant = keep("ln_mant", [P, 8], F32)
+        ln_amp = keep("ln_amp", [P, 8], F32)
+        ss_bf = keep("ss_bf", [P, 8], BF16)
+        ss_sb = keep("ss_sb", [P, N], BF16)
+        z_codes = keep("z_codes", [P, J], U32)
+        z_scales = keep("z_scales", [P, J], U8)
+        x_codes = keep("x_codes", [P, M], U32)
+        x_scales = keep("x_scales", [P, M], U8)
+        w_codes = keep("w_codes", [P, 2, N], U32)
+        w_scales = keep("w_scales", [P, 2, N], U8)
+        k_codes = keep("k_codes", [P, 2, M], U32)
+        k_scales = keep("k_scales", [P, 2, M], U8)
+        y_codes = keep("y_codes", [P, 2, M], U32)
+        y_scales = keep("y_scales", [P, 2, M], U8)
+        ss_bank = ps.tile([P, 512], F32, name="ss_bank", tag="ss_bank")
+        words_out = out_1.rearrange("g p m t -> p g (m t)").bitcast(I32)
+
+        def interleave(eng, dst, src):
+            if FOUR:
+                d = dst.rearrange("p (c i t) -> p c t i", i=4, t=4)
+                s = src.rearrange("p t (c i) -> p c t i", i=4)
+            else:
+                d = dst.rearrange("p (c t) -> p c t", t=4)
+                s = src.rearrange("p t c -> p c t")
+            if eng == "V":
+                nc.vector.tensor_copy(out=d, in_=s)
+            elif eng == "S":
+                nc.scalar.copy(out=d, in_=s)
+            else:
+                nc.gpsimd.tensor_scalar(out=d, in0=s, scalar1=1.0, scalar2=1.0, op0=ALU.mult, op1=ALU.mult)
+
+        def ss_view(c0, c1):
+            return ss_bank[:].bitcast(BF16).rearrange("m (i p e) -> m p i e", i=4, e=2)[:, c0 // 8 : c1 // 8]
+
+        for op in schedule(params()):
+            o, a = op[0], op[1:]
+            if o == "load":
+                if a[0] == "amp":
+                    nc.sync.dma_start(out=amp_bf[:].rearrange("p (g t) -> p g t", g=2), in_=amp.rearrange("(g p t) -> p g t", g=2, t=4))
+                elif a[0] == "ss":
+                    nc.sync.dma_start(out=ss_bf[:], in_=state_scale.rearrange("(p i) -> p i", i=8))
+                elif a[0] == "z":
+                    T[a] = keep("z%d" % a[1], [P, 4, D], BF16)
+                    nc.sync.dma_start(out=T[a][:], in_=z[512 * a[1] : 512 * a[1] + 512, :].rearrange("(r t) d -> r t d", t=4))
+                elif a[0] == "x":
+                    T[a] = keep("x%d" % a[1], [P, 4, D], BF16)
+                    nc.sync.dma_start(out=T[a][:], in_=x[512 * a[1] : 512 * a[1] + 512, :].rearrange("(t r) d -> r t d", t=4))
+                elif a[0] == "w":
+                    T[a] = keep("w%d%d" % a[1:], [P, 4, 512], BF16)
+                    nc.sync.dma_start(out=T[a][:], in_=w[512 * a[1] : 512 * a[1] + 512, 512 * a[2] : 512 * a[2] + 512].rearrange("(p t) c -> p t c", t=4))
+                else:
+                    T[a] = keep("mean%d" % a[1], [P, 2, N], BF16)
+                    nc.sync.dma_start(out=T[a][:], in_=mean[256 * a[1] : 256 * a[1] + 256, :].rearrange("(t r) c -> r t c", t=2))
+            elif o == "consts":
+                make_identity(nc, ident[:])
+                nc.vector.memset(one[:], 1.0)
+                nc.scalar.activation(out=warm[:], in_=one[:], func=ACT.Ln)
+            elif o == "amp_pre":
+                nc.vector.tensor_scalar(out=mant[:], in0=amp_bf[:].bitcast(I32), scalar1=0x007F007F, scalar2=0x3F803F80, op0=ALU.bitwise_and, op1=ALU.bitwise_or)
+                nc.vector.tensor_copy(out=amp32[:], in_=amp_bf[:])
+                nc.vector.tensor_scalar(out=sign2[:], in0=amp_bf[:], scalar1=0.0, scalar2=2.0, op0=ALU.is_ge, op1=ALU.mult)
+                nc.vector.tensor_scalar(out=exp_i[:], in0=amp32[:].bitcast(I32), scalar1=23, scalar2=255, op0=ALU.logical_shift_right, op1=ALU.bitwise_and)
+                nc.vector.tensor_scalar(out=sign[:], in0=sign2[:], scalar1=-1.0, scalar2=None, op0=ALU.add)
+                nc.vector.tensor_copy(out=exp_f[:], in_=exp_i[:])
+                nc.vector.tensor_scalar(out=ln_pow[:], in0=exp_f[:], scalar1=-127.0, scalar2=math.log(2.0), op0=ALU.add, op1=ALU.mult)
+                nc.vector.tensor_scalar(out=dead[:], in0=exp_f[:], scalar1=0.0, scalar2=-2048.0, op0=ALU.is_equal, op1=ALU.mult)
+                nc.vector.tensor_tensor(out=ln_part[:], in0=ln_pow[:], in1=dead[:], op=ALU.add)
+            elif o == "ln":
+                nc.scalar.activation(out=ln_mant[:], in_=mant[:].bitcast(BF16), func=ACT.Ln)
+                nc.scalar.activation(out=warm[:], in_=one[:], func=ACT.Exp)
+            elif o == "amp_post":
+                nc.vector.tensor_tensor(out=ln_amp[:], in0=ln_part[:], in1=ln_mant[:], op=ALU.add)
+            elif o in ("zt", "xt"):
+                bank = rot(ps, "sbank", op, [P, 512], F32)
+                for r in range(2):
+                    words = T[(o[0], a[0])][:, 2 * a[1] + r, :].bitcast(F32)
+                    for u in range(2):
+                        c0 = 256 * r + 128 * u
+                        nc.tensor.transpose(bank[:, c0 : c0 + 128], words[:, u:256:2], ident[:])
+            elif o in ("zc", "xc"):
+                dst = rot(sb, o[0] + "i", (o[0] + "i", a[0]), [P, 2048], BF16)
+                bank = T[(o[0] + "t",) + a]
+                nc.scalar.copy(
+                    out=dst[:, 1024 * a[1] : 1024 * a[1] + 1024].bitcast(F32).rearrange("p (r m u) -> p r m u", r=2, u=2),
+                    in_=bank[:].rearrange("p (r u m) -> p r m u", r=2, u=2),
+                )
+            elif o in ("zq", "xq"):
+                codes, scales = (z_codes, z_scales) if o == "zq" else (x_codes, x_scales)
+                cols = slice(512 * a[0], 512 * a[0] + 512)
+                nc.vector.quantize_mx(out=codes[:, cols].bitcast(FP8X4), scales=scales[:, cols], in_=T[(o[0] + "i", a[0])][:])
+            elif o == "sst":
+                words = ss_bf[:].bitcast(F32)
+                for i in range(4):
+                    nc.tensor.transpose(ss_bank[:, 128 * i : 128 * i + 128], words[:, i : i + 1].to_broadcast([P, P]), ident[:])
+            elif o == "ssc":
+                for h in range(2):
+                    nc.scalar.copy(out=ss_sb[:, 512 * h : 512 * h + 512].rearrange("m (p i e) -> m p i e", i=4, e=2), in_=ss_view(512 * h, 512 * h + 512))
+            elif o == "ws":
+                dst = rot(sb, "wsg", op, [P, 4, 512], BF16)
+                for t in range(4):
+                    col = 4 * a[0] + t
+                    nc.vector.tensor_scalar(out=dst[:, t, :], in0=T[("w",) + a][:, t, :], scalar1=sign[:, col : col + 1], scalar2=None, op0=ALU.mult)
+            elif o == "wi":
+                dst = rot(sb, a[3] if len(a) > 3 else "wil", ("wi",) + a[:2], [P, 2048], BF16)
+                interleave(a[2], dst[:], T[("ws",) + a[:2]][:])
+            elif o == "wq":
+                cols = slice(512 * a[1], 512 * a[1] + 512)
+                nc.vector.quantize_mx(out=w_codes[:, a[0], cols].bitcast(FP8X4), scales=w_scales[:, a[0], cols], in_=T[("wi",) + a][:])
+            elif o == "s1":
+                k, g, t = a
+                bank = rot(ps, "sbank", op, [P, 512], F32)
+                jc = slice(512 * g + 128 * t, 512 * g + 128 * t + 128)
+                mc = slice(512 * k, 512 * k + 512)
+                nc.tensor.matmul_mx(out=bank[:], lhsT=z_codes[:, jc].bitcast(FP8X4), lhsT_scale=z_scales[:, jc], rhs=x_codes[:, mc].bitcast(FP8X4), rhs_scale=x_scales[:, mc], start=True, stop=True)
+            elif o == "ex":
+                k, g, t = a
+                dst = rot(sb, "ez", ("ez", k, g), [P, 4, 512], BF16)
+                col = 4 * g + t
+                nc.scalar.activation(out=dst[:, t, :], in_=T[("s1",) + a][:], func=ACT.Exp, bias=ln_amp[:, col : col + 1])
+            elif o == "ki":
+                k, g, hf, m0, m1, eng, tag = a
+                dst = rot(sb, tag, ("ki", k, g, hf), [P, 1024], BF16)
+                interleave(eng, dst[:, 4 * m0 : 4 * m1], T[("ez", k, g)][:, :, 256 * hf + m0 : 256 * hf + m1])
+            elif o == "kq":
+                k, g, hf = a
+                cols = slice(512 * k + 256 * hf, 512 * k + 256 * hf + 256)
+                nc.vector.quantize_mx(out=k_codes[:, g, cols].bitcast(FP8X4), scales=k_scales[:, g, cols], in_=T[("ki",) + a][:])
+            elif o == "s2":
+                i, h = a
+                bank = rot(ps, "s2bank", op, [P, 512], F32)
+                mc = slice(128 * i, 128 * i + 128)
+                cc = slice(512 * h, 512 * h + 512)
+                for g in range(2):
+                    nc.tensor.matmul_mx(out=bank[:], lhsT=k_codes[:, g, mc].bitcast(FP8X4), lhsT_scale=k_scales[:, g, mc], rhs=w_codes[:, g, cc].bitcast(FP8X4), rhs_scale=w_scales[:, g, cc], start=(g == 0), stop=(g == 1))
+            elif o == "ad":
+                i, h = a
+                dst = rot(sb, "tmp", ("tmp", i), [P, N], F32)
+                cc = slice(512 * h, 512 * h + 512)
+                nc.vector.tensor_tensor(out=dst[:, cc], in0=T[("s2", i, h)][:], in1=T[("mean", i // 2)][:, i % 2, cc], op=ALU.add)
+            elif o == "mu":
+                i, c0, c1, eng = a
+                dst = rot(sb, "y", ("y", i), [P, N], F32)
+                cc = slice(c0, c1)
+                if eng == "G":
+                    nc.gpsimd.tensor_tensor(out=dst[:, cc], in0=T[("tmp", i)][:, cc], in1=ss_sb[:, cc], op=ALU.mult)
+                else:
+                    nc.vector.tensor_tensor(
+                        out=dst[:, cc].rearrange("m (p i e) -> m p i e", i=4, e=2),
+                        in0=T[("tmp", i)][:, cc].rearrange("m (p i e) -> m p i e", i=4, e=2),
+                        in1=ss_view(c0, c1),
+                        op=ALU.mult,
+                    )
+            elif o == "sty":
+                i = a[0]
+                cc = slice(0, N) if len(a) == 1 else slice(512 * a[1], 512 * a[1] + 512)
+                nc.sync.dma_start(out=out_0[128 * i : 128 * i + 128, cc], in_=T[("y", i)][:, cc])
+            elif o == "ca":
+                i, q0, q1, eng = a
+                dst = rot(sb, "yc", ("yc", i), [P, N], BF16)
+                d = dst[:].rearrange("m (u q e) -> m u q e", u=2, e=2)[:, :, q0:q1, :]
+                s = T[("y", i)][:].rearrange("m (q u e) -> m u q e", u=2, e=2)[:, :, q0:q1, :]
+                if eng == "V":
+                    nc.vector.tensor_copy(out=d, in_=s)
+                elif eng == "S":
+                    nc.scalar.copy(out=d, in_=s)
+                else:
+                    nc.gpsimd.tensor_scalar(out=d, in0=s, scalar1=1.0, scalar2=1.0, op0=ALU.mult, op1=ALU.mult)
+            elif o == "yt":
+                i = a[0]
+                bank = rot(ps, "sbank", op, [P, 512], F32)
+                words = T[("yc", i)][:].bitcast(F32)
+                for g in (range(2) if len(a) == 1 else [a[1]]):
+                    for u in range(2):
+                        c0, w0 = 256 * g + 128 * u, 256 * u + 128 * g
+                        nc.tensor.transpose(bank[:, c0 : c0 + 128], words[:, w0 : w0 + 128], ident[:])
+            elif o == "yw":
+                i = a[0]
+                dst = rot(sb, "yi", ("yi", i), [P, N], BF16)
+                gs = slice(0, 2) if len(a) == 1 else slice(a[1], a[1] + 1)
+                nc.scalar.copy(
+                    out=dst[:].bitcast(F32).rearrange("p (g m u) -> p g m u", g=2, u=2)[:, gs],
+                    in_=T[("yt",) + a][:].rearrange("p (g u m) -> p g m u", g=2, u=2)[:, gs],
+                )
+            elif o == "yq":
+                i, g = a
+                mc = slice(128 * i, 128 * i + 128)
+                nc.vector.quantize_mx(out=y_codes[:, g, mc].bitcast(FP8X4), scales=y_scales[:, g, mc], in_=T[("yi", i)][:, 512 * g : 512 * g + 512])
+            elif o == "stw":
+                mc = slice(128 * a[0], 128 * a[1])
+                nc.sync.dma_start(out=words_out[:, :, mc], in_=y_codes[:, :, mc].bitcast(I32))
+            elif o == "sts":
+                mc = slice(128 * a[0], 128 * a[1])
+                for q in range(4):
+                    eng = nc.scalar if (a[1] == 16 and q >= 2) else nc.sync
+                    eng.dma_start(
+                        out=out_2[:, 4 * q : 4 * q + 4, mc].rearrange("g r m -> r g m").bitcast(I32),
+                        in_=y_scales[32 * q : 32 * q + 4, :, mc].bitcast(I32),
+                    )
+            else:
+                raise ValueError(o)

@@ -17,9 +17,9 @@ ALU = mybir.AluOpType
 ACT = mybir.ActivationFunctionType
 
 BUFS = dict(sbank=4, s2bank=3, kzi=1, kzv=3, ez=3, y=4, tmp=2, yc=2, yi=2, wsg=4, wil=2, xi=2, zi=2)
-FOUR = False
-GM = {9: 256, 10: 320, 11: 320, 12: 320, 13: 448, 14: 448}
-GC = dict((s, 80) for s in range(1, 9))
+FOUR = "VS"
+GM = {9: 256, 10: 256, 11: 256, 12: 256, 13: 384, 14: 384}
+GC = dict((s, 64) for s in range(3, 9))
 GK = {9: 128, 10: 128, 11: 128, 12: 128}
 
 
@@ -32,9 +32,7 @@ def schedule(P):
     for l in P["loads"]:
         add("load", *l)
     add("consts")
-    add("amp_pre")
-    add("ln")
-    add("amp_post")
+    add("vt")
     for op in P["head"]:
         add(*op)
     S = 16
@@ -75,53 +73,55 @@ def schedule(P):
             add("ex", *op)
         for op in P["sk"].get(s, []):
             add(*op)
-        if s >= 2:
-            add("yq", s - 2, 0)
-            add("yq", s - 2, 1)
-            if (s - 2) % 4 == 3:
-                add("stw", s - 5, s - 1)
-            if s - 2 == 11:
-                add("sts", 0, 12)
         for op in P["vq"].get(s, []):
             add(*op)
+        if s >= 3:
+            j, g = (s - 3) // 2, (s - 3) % 2
+            add("yq", 2 * j, 2 * j + 2, g)
+            if g == 1 and j % 2 == 1:
+                add("stw", 2 * j - 2, 2 * j + 2)
+            if g == 1 and j == 5:
+                add("sts", 0, 12)
     add("yt", 14)
     add("ca", 15, 0, 128, "S")
     add("yw", 14)
+    add("yq", 12, 14, 1)
+    add("stw", 12, 14)
     add("ca", 15, 128, 256, "V")
     add("yt", 15, 0)
     add("yt", 15, 1)
-    add("yq", 14, 0)
-    add("yq", 14, 1)
-    add("stw", 12, 15)
     add("yw", 15, 0)
     add("yw", 15, 1)
-    add("yq", 15, 0)
-    add("yq", 15, 1)
-    add("stw", 15, 16)
+    add("yq", 14, 16, 0)
+    add("yq", 14, 16, 1)
+    add("stw", 14, 16)
     add("sts", 12, 16)
     return ops
 
 
 def params():
     P = {}
-    P["loads"] = [("amp",), ("z", 0), ("w", 0, 0), ("x", 0), ("w", 1, 0), ("z", 1), ("ss",), ("w", 0, 1), ("w", 1, 1), ("x", 1), ("mean", 0), ("mean", 1), ("x", 2), ("mean", 2), ("mean", 3), ("x", 3)] + [("mean", i) for i in range(4, 8)]
+    P["loads"] = [("z", 0, 0), ("w", 0, 0), ("z", 0, 1), ("x", 0), ("w", 1, 0), ("w", 0, 1), ("z", 1, 0), ("z", 1, 1), ("x", 1), ("w", 1, 1), ("x", 2), ("mean", 0), ("mean", 1), ("x", 3)] + [("mean", i) for i in range(2, 8)]
     H = []
-    H += [("zt", 0, 0), ("zt", 0, 1), ("zc", 0, 0), ("zc", 0, 1)]
-    H += [("ws", 0, 0), ("wi", 0, 0, "V"), ("zq", 0)]
-    H += [("xt", 0, 0), ("xt", 0, 1), ("xc", 0, 0), ("xc", 0, 1)]
-    H += [("ws", 1, 0), ("wi", 1, 0, "S"), ("wq", 0, 0), ("xq", 0)]
-    H += [("zt", 1, 0), ("zt", 1, 1)]
-    H += [("s1", 0, 0, 0), ("s1", 0, 0, 1), ("zc", 1, 0), ("zc", 1, 1), ("ex", 0, 0, 0), ("ex", 0, 0, 1)]
-    H += [("ws", 0, 1), ("wi", 0, 1, "V"), ("wq", 1, 0), ("zq", 1), ("ws", 1, 1), ("wq", 0, 1), ("wi", 1, 1, "V")]
-    for t in range(2, 4):
+    ws = lambda g, h: [("ws", g, h, t) for t in range(4)]
+    H += [("am", 0), ("am", 1), ("am", 3), ("am", 2), ("am", 4), ("zt", 0, 0), ("zc", 0, 0), ("zt", 0, 1), ("zc", 0, 1), ("ln",)]
+    for t in range(4):
+        H += [("ws", 0, 0, t)] + [("am", 5 + t)] * (t < 3)
+    H += [("wi", 0, 0, "V"), ("zq", 0), ("wq", 0, 0)]
+    H += [("xt", 0, 0), ("xt", 0, 1), ("xc", 0, 0), ("xc", 0, 1), ("sst",)]
+    H += ws(1, 0) + [("am", 8), ("wi", 1, 0, "S"), ("xq", 0)] + ws(0, 1) + [("wi", 0, 1, "V"), ("wq", 1, 0)]
+    H += [("zt", 1, 0), ("zt", 1, 1), ("zc", 1, 0), ("zc", 1, 1)]
+    for t in range(4):
         H += [("s1", 0, 0, t), ("ex", 0, 0, t)]
-    H += [("xt", 1, 0), ("xt", 1, 1), ("sst",), ("xc", 1, 0), ("xc", 1, 1)]
+    H += [("wq", 0, 1), ("zq", 1)] + ws(1, 1) + [("wi", 1, 1, "V")]
+    H += [("xt", 1, 0), ("xt", 1, 1), ("xc", 1, 0), ("xc", 1, 1)]
     for t in range(4):
         H += [("s1", 0, 1, t), ("ex", 0, 1, t)]
-    H += [("xq", 1), ("ki", 0, 0, 0, 0, 256, "V", "kzv"), ("wq", 1, 1), ("ki", 0, 0, 1, 0, 256, "V", "kzi"), ("kq", 0, 0, 0), ("ki", 0, 1, 0, 0, 256, "V", "kzv"), ("kq", 0, 1, 0), ("kq", 0, 0, 1)]
-    for t in range(3):
+    H += [("xt", 2, 0), ("xt", 2, 1), ("xc", 2, 0), ("xc", 2, 1)]
+    H += [("ki", 0, 0, 0, 0, 256, "V", "kzv"), ("ki", 0, 0, 1, 0, 256, "V", "kzi"), ("wq", 1, 1), ("kq", 0, 0, 0), ("xq", 1), ("ki", 0, 1, 0, 0, 256, "V", "kzv"), ("kq", 0, 1, 0), ("xq", 2), ("kq", 0, 0, 1)]
+    for t in range(4):
         H += [("s1", 1, 0, t), ("ex", 1, 0, t)]
-    H += [("s2", 0, 0), ("s2", 0, 1), ("s1", 1, 0, 3), ("ex", 1, 0, 3)]
+    H += [("s2", 0, 0), ("s1", 1, 1, 0), ("ex", 1, 1, 0), ("s2", 0, 1), ("s1", 1, 1, 1), ("ex", 1, 1, 1)]
     P["head"] = H
     P["g"], P["vq"], P["ex"], P["xt"], P["xc"], P["sk"] = {}, {}, {}, {}, {}, {}
     P["g"][0] = [("ki", 0, 1, 1, 0, 256, "G", "kzi")]
@@ -134,15 +134,12 @@ def params():
             if m1 < 256:
                 P["g"][s].append(("ki", k, g, hf, m1, 256, "S", "kzi"))
             P["vq"].setdefault(s, []).append(("kq", k, g, hf))
-    P["ex"][0] = [(1, 1, t) for t in range(4)]
+    P["ex"][0] = [(1, 1, t) for t in range(2, 4)]
     for k in (2, 3):
         s0 = 4 * k - 7
         for n in range(4):
             P["ex"].setdefault(s0 + n, []).extend([(k, n // 2, 2 * (n % 2)), (k, n // 2, 2 * (n % 2) + 1)])
-    P["xt"][0] = [("xt", 2, 0), ("xt", 2, 1)]
-    P["xc"][0] = [("xc", 2, 0), ("xc", 2, 1)]
-    P["vq"][0].insert(0, ("xq", 2))
-    P["sk"][7] = [("ssc",)]
+    P["sk"][5] = [("ssc",)]
     for n in range(2):
         P["xt"][3 + n] = [("xt", 3, n)]
         P["xc"][3 + n] = [("xc", 3, n)]
@@ -176,15 +173,14 @@ def tile_inducing_kernel_mean_h3_kernel(tc, x, z, amp, w, mean, state_scale, out
         ident = keep("ident", [P, P], F32)
         one = keep("one", [P, 1], F32)
         warm = keep("warm", [P, 1], F32)
+        rows = keep("rows", [P, 256], F32)
         amp_bf = keep("amp_bf", [P, 8], BF16)
         mant = keep("mant", [P, 4], I32)
-        amp32 = keep("amp32", [P, 8], F32)
         exp_i = keep("exp_i", [P, 8], I32)
         exp_f = keep("exp_f", [P, 8], F32)
         sign2 = keep("sign2", [P, 8], F32)
         sign = keep("sign", [P, 8], F32)
         dead = keep("dead", [P, 8], F32)
-        ln_pow = keep("ln_pow", [P, 8], F32)
         ln_part = keep("ln_part", [P, 8], F32)
         ln_mant = keep("ln_mant", [P, 8], F32)
         ln_amp = keep("ln_amp", [P, 8], F32)
@@ -204,7 +200,7 @@ def tile_inducing_kernel_mean_h3_kernel(tc, x, z, amp, w, mean, state_scale, out
         words_out = out_1.rearrange("g p m t -> p g (m t)").bitcast(I32)
 
         def interleave(eng, dst, src):
-            if FOUR:
+            if eng in FOUR:
                 d = dst.rearrange("p (c i t) -> p c t i", i=4, t=4)
                 s = src.rearrange("p t (c i) -> p c t i", i=4)
             else:
@@ -218,21 +214,19 @@ def tile_inducing_kernel_mean_h3_kernel(tc, x, z, amp, w, mean, state_scale, out
                 nc.gpsimd.tensor_scalar(out=d, in0=s, scalar1=1.0, scalar2=1.0, op0=ALU.mult, op1=ALU.mult)
 
         def ss_view(c0, c1):
-            return ss_bank[:].bitcast(BF16).rearrange("m (i p e) -> m p i e", i=4, e=2)[:, c0 // 8 : c1 // 8]
+            return ss_bank[:].bitcast(BF16)[:, c0:c1]
 
         for op in schedule(params()):
             o, a = op[0], op[1:]
             if o == "load":
-                if a[0] == "amp":
-                    nc.sync.dma_start(out=amp_bf[:].rearrange("p (g t) -> p g t", g=2), in_=amp.rearrange("(g p t) -> p g t", g=2, t=4))
-                elif a[0] == "ss":
-                    nc.sync.dma_start(out=ss_bf[:], in_=state_scale.rearrange("(p i) -> p i", i=8))
-                elif a[0] == "z":
-                    T[a] = keep("z%d" % a[1], [P, 4, D], BF16)
-                    nc.sync.dma_start(out=T[a][:], in_=z[512 * a[1] : 512 * a[1] + 512, :].rearrange("(r t) d -> r t d", t=4))
+                if a[0] == "z":
+                    if ("z", a[1]) not in T:
+                        T[("z", a[1])] = keep("z%d" % a[1], [P, 4, D], BF16)
+                    ts = slice(2 * a[2], 2 * a[2] + 2)
+                    nc.sync.dma_start(out=T[("z", a[1])][:, ts, :], in_=z[512 * a[1] : 512 * a[1] + 512, :].rearrange("(r t) d -> r t d", t=4)[:, ts, :])
                 elif a[0] == "x":
                     T[a] = keep("x%d" % a[1], [P, 4, D], BF16)
-                    nc.sync.dma_start(out=T[a][:], in_=x[512 * a[1] : 512 * a[1] + 512, :].rearrange("(t r) d -> r t d", t=4))
+                    nc.sync.dma_start(out=T[a][:].rearrange("r (a e) d -> r a e d", e=2), in_=x[512 * a[1] : 512 * a[1] + 512, :].rearrange("(a r e) d -> r a e d", a=2, e=2))
                 elif a[0] == "w":
                     T[a] = keep("w%d%d" % a[1:], [P, 4, 512], BF16)
                     nc.sync.dma_start(out=T[a][:], in_=w[512 * a[1] : 512 * a[1] + 512, 512 * a[2] : 512 * a[2] + 512].rearrange("(p t) c -> p t c", t=4))
@@ -240,24 +234,43 @@ def tile_inducing_kernel_mean_h3_kernel(tc, x, z, amp, w, mean, state_scale, out
                     T[a] = keep("mean%d" % a[1], [P, 2, N], BF16)
                     nc.sync.dma_start(out=T[a][:], in_=mean[256 * a[1] : 256 * a[1] + 256, :].rearrange("(t r) c -> r t c", t=2))
             elif o == "consts":
+                nc.vector.memset(rows[:], 0.0)
+                nc.scalar.dma_start(out=rows[0:2, :].bitcast(BF16), in_=amp.rearrange("(g c) -> g c", g=2))
+                nc.scalar.dma_start(out=rows[2:4, :].bitcast(BF16), in_=state_scale.rearrange("(g c) -> g c", g=2))
                 make_identity(nc, ident[:])
                 nc.vector.memset(one[:], 1.0)
                 nc.scalar.activation(out=warm[:], in_=one[:], func=ACT.Ln)
-            elif o == "amp_pre":
-                nc.vector.tensor_scalar(out=mant[:], in0=amp_bf[:].bitcast(I32), scalar1=0x007F007F, scalar2=0x3F803F80, op0=ALU.bitwise_and, op1=ALU.bitwise_or)
-                nc.vector.tensor_copy(out=amp32[:], in_=amp_bf[:])
-                nc.vector.tensor_scalar(out=sign2[:], in0=amp_bf[:], scalar1=0.0, scalar2=2.0, op0=ALU.is_ge, op1=ALU.mult)
-                nc.vector.tensor_scalar(out=exp_i[:], in0=amp32[:].bitcast(I32), scalar1=23, scalar2=255, op0=ALU.logical_shift_right, op1=ALU.bitwise_and)
-                nc.vector.tensor_scalar(out=sign[:], in0=sign2[:], scalar1=-1.0, scalar2=None, op0=ALU.add)
-                nc.vector.tensor_copy(out=exp_f[:], in_=exp_i[:])
-                nc.vector.tensor_scalar(out=ln_pow[:], in0=exp_f[:], scalar1=-127.0, scalar2=math.log(2.0), op0=ALU.add, op1=ALU.mult)
-                nc.vector.tensor_scalar(out=dead[:], in0=exp_f[:], scalar1=0.0, scalar2=-2048.0, op0=ALU.is_equal, op1=ALU.mult)
-                nc.vector.tensor_tensor(out=ln_part[:], in0=ln_pow[:], in1=dead[:], op=ALU.add)
+            elif o == "vt":
+                bank = rot(ps, "sbank", op, [P, 512], F32)
+                for u in range(2):
+                    nc.tensor.transpose(bank[:, 128 * u : 128 * u + 128], rows[:, u:256:2], ident[:])
+                for u in range(2):
+                    nc.tensor.transpose(bank[:, 256 + 128 * u : 384 + 128 * u], rows[:, 128 * u : 128 * u + 128], ident[:])
+                view = bank[:].rearrange("p (k r) -> p r k", k=4)
+                nc.vector.tensor_copy(out=amp_bf[:].bitcast(F32).rearrange("p (g u) -> p g u", g=2), in_=view[:, 0:2, 0:2])
+                nc.vector.tensor_copy(out=ss_bf[:].bitcast(F32).rearrange("p (g u) -> p g u", g=2), in_=view[:, 2:4, 2:4])
+            elif o == "am":
+                words = amp_bf[:].bitcast(I32)
+                if a[0] == 0:
+                    nc.vector.tensor_scalar(out=sign2[:], in0=amp_bf[:], scalar1=0.0, scalar2=2.0, op0=ALU.is_ge, op1=ALU.mult)
+                elif a[0] == 1:
+                    nc.vector.tensor_scalar(out=mant[:], in0=words, scalar1=0x007F007F, scalar2=0x3F803F80, op0=ALU.bitwise_and, op1=ALU.bitwise_or)
+                elif a[0] == 2:
+                    nc.vector.tensor_scalar(out=sign[:], in0=sign2[:], scalar1=-1.0, scalar2=None, op0=ALU.add)
+                elif a[0] in (3, 4):
+                    e = a[0] - 3
+                    nc.vector.tensor_scalar(out=exp_i[:, e:8:2], in0=words, scalar1=7 + 16 * e, scalar2=255, op0=ALU.logical_shift_right, op1=ALU.bitwise_and)
+                elif a[0] == 5:
+                    nc.vector.tensor_copy(out=exp_f[:], in_=exp_i[:])
+                elif a[0] == 6:
+                    nc.vector.tensor_scalar(out=dead[:], in0=exp_f[:], scalar1=0.0, scalar2=-4096.0, op0=ALU.is_equal, op1=ALU.mult)
+                elif a[0] == 7:
+                    nc.vector.scalar_tensor_tensor(out=ln_part[:], in0=exp_f[:], scalar=-127.0, in1=dead[:], op0=ALU.add, op1=ALU.add)
+                else:
+                    nc.vector.scalar_tensor_tensor(out=ln_amp[:], in0=ln_part[:], scalar=math.log(2.0), in1=ln_mant[:], op0=ALU.mult, op1=ALU.add)
             elif o == "ln":
                 nc.scalar.activation(out=ln_mant[:], in_=mant[:].bitcast(BF16), func=ACT.Ln)
                 nc.scalar.activation(out=warm[:], in_=one[:], func=ACT.Exp)
-            elif o == "amp_post":
-                nc.vector.tensor_tensor(out=ln_amp[:], in0=ln_part[:], in1=ln_mant[:], op=ALU.add)
             elif o in ("zt", "xt"):
                 bank = rot(ps, "sbank", op, [P, 512], F32)
                 for r in range(2):
@@ -268,10 +281,11 @@ def tile_inducing_kernel_mean_h3_kernel(tc, x, z, amp, w, mean, state_scale, out
             elif o in ("zc", "xc"):
                 dst = rot(sb, o[0] + "i", (o[0] + "i", a[0]), [P, 2048], BF16)
                 bank = T[(o[0] + "t",) + a]
-                nc.scalar.copy(
-                    out=dst[:, 1024 * a[1] : 1024 * a[1] + 1024].bitcast(F32).rearrange("p (r m u) -> p r m u", r=2, u=2),
-                    in_=bank[:].rearrange("p (r u m) -> p r m u", r=2, u=2),
-                )
+                words = dst[:, 1024 * a[1] : 1024 * a[1] + 1024].bitcast(F32)
+                if o == "zc":
+                    nc.scalar.copy(out=words.rearrange("p (r m u) -> p r m u", r=2, u=2), in_=bank[:].rearrange("p (r u m) -> p r m u", r=2, u=2))
+                else:
+                    nc.scalar.copy(out=words.rearrange("p (m k) -> p m k", k=4), in_=bank[:].rearrange("p (k m) -> p m k", k=4))
             elif o in ("zq", "xq"):
                 codes, scales = (z_codes, z_scales) if o == "zq" else (x_codes, x_scales)
                 cols = slice(512 * a[0], 512 * a[0] + 512)
@@ -281,13 +295,11 @@ def tile_inducing_kernel_mean_h3_kernel(tc, x, z, amp, w, mean, state_scale, out
                 for i in range(4):
                     nc.tensor.transpose(ss_bank[:, 128 * i : 128 * i + 128], words[:, i : i + 1].to_broadcast([P, P]), ident[:])
             elif o == "ssc":
-                for h in range(2):
-                    nc.scalar.copy(out=ss_sb[:, 512 * h : 512 * h + 512].rearrange("m (p i e) -> m p i e", i=4, e=2), in_=ss_view(512 * h, 512 * h + 512))
+                nc.scalar.copy(out=ss_sb[:, 0:512], in_=ss_view(0, 512))
             elif o == "ws":
-                dst = rot(sb, "wsg", op, [P, 4, 512], BF16)
-                for t in range(4):
-                    col = 4 * a[0] + t
-                    nc.vector.tensor_scalar(out=dst[:, t, :], in0=T[("w",) + a][:, t, :], scalar1=sign[:, col : col + 1], scalar2=None, op0=ALU.mult)
+                g, h, t = a
+                dst = rot(sb, "wsg", ("ws", g, h), [P, 4, 512], BF16)
+                nc.vector.tensor_scalar(out=dst[:, t, :], in0=T[("w", g, h)][:, t, :], scalar1=sign[:, 4 * g + t : 4 * g + t + 1], scalar2=None, op0=ALU.mult)
             elif o == "wi":
                 dst = rot(sb, a[3] if len(a) > 3 else "wil", ("wi",) + a[:2], [P, 2048], BF16)
                 interleave(a[2], dst[:], T[("ws",) + a[:2]][:])
@@ -332,12 +344,7 @@ def tile_inducing_kernel_mean_h3_kernel(tc, x, z, amp, w, mean, state_scale, out
                 if eng == "G":
                     nc.gpsimd.tensor_tensor(out=dst[:, cc], in0=T[("tmp", i)][:, cc], in1=ss_sb[:, cc], op=ALU.mult)
                 else:
-                    nc.vector.tensor_tensor(
-                        out=dst[:, cc].rearrange("m (p i e) -> m p i e", i=4, e=2),
-                        in0=T[("tmp", i)][:, cc].rearrange("m (p i e) -> m p i e", i=4, e=2),
-                        in1=ss_view(c0, c1),
-                        op=ALU.mult,
-                    )
+                    nc.vector.tensor_tensor(out=dst[:, cc], in0=T[("tmp", i)][:, cc], in1=ss_view(c0, c1), op=ALU.mult)
             elif o == "sty":
                 i = a[0]
                 cc = slice(0, N) if len(a) == 1 else slice(512 * a[1], 512 * a[1] + 512)
@@ -363,16 +370,16 @@ def tile_inducing_kernel_mean_h3_kernel(tc, x, z, amp, w, mean, state_scale, out
                         nc.tensor.transpose(bank[:, c0 : c0 + 128], words[:, w0 : w0 + 128], ident[:])
             elif o == "yw":
                 i = a[0]
-                dst = rot(sb, "yi", ("yi", i), [P, N], BF16)
+                dst = rot(sb, "yi", ("yi", i // 2), [P, 2, 1024], BF16)
                 gs = slice(0, 2) if len(a) == 1 else slice(a[1], a[1] + 1)
                 nc.scalar.copy(
-                    out=dst[:].bitcast(F32).rearrange("p (g m u) -> p g m u", g=2, u=2)[:, gs],
+                    out=dst[:, gs, 512 * (i % 2) : 512 * (i % 2) + 512].bitcast(F32).rearrange("p g (m u) -> p g m u", u=2),
                     in_=T[("yt",) + a][:].rearrange("p (g u m) -> p g m u", g=2, u=2)[:, gs],
                 )
             elif o == "yq":
-                i, g = a
-                mc = slice(128 * i, 128 * i + 128)
-                nc.vector.quantize_mx(out=y_codes[:, g, mc].bitcast(FP8X4), scales=y_scales[:, g, mc], in_=T[("yi", i)][:, 512 * g : 512 * g + 512])
+                i0, i1, g = a
+                mc = slice(128 * i0, 128 * i1)
+                nc.vector.quantize_mx(out=y_codes[:, g, mc].bitcast(FP8X4), scales=y_scales[:, g, mc], in_=T[("yi", i0 // 2)][:, g, 512 * (i0 % 2) : 512 * (i0 % 2) + 512 * (i1 - i0)])
             elif o == "stw":
                 mc = slice(128 * a[0], 128 * a[1])
                 nc.sync.dma_start(out=words_out[:, :, mc], in_=y_codes[:, :, mc].bitcast(I32))

@@ -16,11 +16,14 @@ FP8X4 = mybir.dt.float8_e4m3fn_x4
 ALU = mybir.AluOpType
 ACT = mybir.ActivationFunctionType
 
-BUFS = dict(sbank=4, s2bank=3, kzi=1, kzv=3, ez=3, y=4, tmp=2, yc=2, yi=2, wsg=4, wil=2, xi=2, zi=2)
+BUFS = dict(sbank=4, s2bank=3, kzi=1, kzv=3, ez=3, y=5, tmp=2, yc=3, yi=3, wsg=4, wil=2, xi=2, zi=2)
 FOUR = "VS"
-GM = {9: 256, 10: 256, 11: 256, 12: 256, 13: 384, 14: 384}
-GC = dict((s, 64) for s in range(3, 9))
+GM = dict((s, 320) for s in range(9, 15))
+GC = dict((s, 64) for s in range(5, 9))
 GK = {9: 128, 10: 128, 11: 128, 12: 128}
+X3, X3Q, SSC = 2, 4, 5
+YQ = dict([(s, [s - 4]) for s in range(4, 13)] + [(13, [9, 10]), (14, [11]), (15, [12])])
+EX0 = {2: 1, 3: 5}
 
 
 def schedule(P):
@@ -29,9 +32,9 @@ def schedule(P):
     def add(*op):
         ops.append(op)
 
+    add("consts")
     for l in P["loads"]:
         add("load", *l)
-    add("consts")
     add("vt")
     for op in P["head"]:
         add(*op)
@@ -41,9 +44,9 @@ def schedule(P):
             add(*op)
         add("ad", s, 0)
         add("ad", s, 1)
-        if s in GC:
+        if GC.get(s, 0):
             add("ca", s - 1, 0, GC[s], "G")
-        if s in GM:
+        if GM.get(s, 0):
             add("mu", s, 0, GM[s], "G")
             add("mu", s, GM[s], 512, "V")
         else:
@@ -75,8 +78,8 @@ def schedule(P):
             add(*op)
         for op in P["vq"].get(s, []):
             add(*op)
-        if s >= 3:
-            j, g = (s - 3) // 2, (s - 3) % 2
+        for n in YQ.get(s, []):
+            j, g = divmod(n, 2)
             add("yq", 2 * j, 2 * j + 2, g)
             if g == 1 and j % 2 == 1:
                 add("stw", 2 * j - 2, 2 * j + 2)
@@ -85,23 +88,25 @@ def schedule(P):
     add("yt", 14)
     add("ca", 15, 0, 128, "S")
     add("yw", 14)
-    add("yq", 12, 14, 1)
-    add("stw", 12, 14)
     add("ca", 15, 128, 256, "V")
+    add("yq", 12, 14, 1)
     add("yt", 15, 0)
     add("yt", 15, 1)
+    add("yq", 14, 15, 0)
+    add("yq", 14, 15, 1)
+    add("stw", 12, 15)
     add("yw", 15, 0)
     add("yw", 15, 1)
-    add("yq", 14, 16, 0)
-    add("yq", 14, 16, 1)
-    add("stw", 14, 16)
+    add("yq", 15, 16, 0)
+    add("yq", 15, 16, 1)
+    add("stw", 15, 16)
     add("sts", 12, 16)
     return ops
 
 
 def params():
     P = {}
-    P["loads"] = [("z", 0, 0), ("w", 0, 0), ("z", 0, 1), ("x", 0), ("w", 1, 0), ("w", 0, 1), ("z", 1, 0), ("z", 1, 1), ("x", 1), ("w", 1, 1), ("x", 2), ("mean", 0), ("mean", 1), ("x", 3)] + [("mean", i) for i in range(2, 8)]
+    P["loads"] = [("z", 0, 0), ("z", 0, 1), ("w", 0, 0), ("x", 0), ("w", 1, 0), ("w", 0, 1), ("z", 1, 0), ("z", 1, 1), ("x", 1), ("w", 1, 1), ("x", 2), ("mean", 0), ("mean", 1), ("x", 3)] + [("mean", i) for i in range(2, 8)]
     H = []
     ws = lambda g, h: [("ws", g, h, t) for t in range(4)]
     H += [("am", 0), ("am", 1), ("am", 3), ("am", 2), ("am", 4), ("zt", 0, 0), ("zc", 0, 0), ("zt", 0, 1), ("zc", 0, 1), ("ln",)]
@@ -130,20 +135,22 @@ def params():
         for n, (g, hf) in enumerate([(0, 0), (1, 0), (0, 1), (1, 1)]):
             s = 4 * k - 3 + n
             m1 = GK.get(s, 256)
-            P["g"].setdefault(s, []).append(("ki", k, g, hf, 0, m1, "G", "kzi"))
+            P["g"].setdefault(s, [])
+            if m1 > 0:
+                P["g"][s].append(("ki", k, g, hf, 0, m1, "G", "kzi"))
             if m1 < 256:
                 P["g"][s].append(("ki", k, g, hf, m1, 256, "S", "kzi"))
             P["vq"].setdefault(s, []).append(("kq", k, g, hf))
     P["ex"][0] = [(1, 1, t) for t in range(2, 4)]
     for k in (2, 3):
-        s0 = 4 * k - 7
+        s0 = EX0[k]
         for n in range(4):
             P["ex"].setdefault(s0 + n, []).extend([(k, n // 2, 2 * (n % 2)), (k, n // 2, 2 * (n % 2) + 1)])
-    P["sk"][5] = [("ssc",)]
+    P["sk"][SSC] = [("ssc",)]
     for n in range(2):
-        P["xt"][3 + n] = [("xt", 3, n)]
-        P["xc"][3 + n] = [("xc", 3, n)]
-    P["vq"][4].insert(0, ("xq", 3))
+        P["xt"][X3 + n] = [("xt", 3, n)]
+        P["xc"][X3 + n] = [("xc", 3, n)]
+    P["vq"][X3Q].insert(0, ("xq", 3))
     return P
 
 
@@ -234,9 +241,9 @@ def tile_inducing_kernel_mean_h3_kernel(tc, x, z, amp, w, mean, state_scale, out
                     T[a] = keep("mean%d" % a[1], [P, 2, N], BF16)
                     nc.sync.dma_start(out=T[a][:], in_=mean[256 * a[1] : 256 * a[1] + 256, :].rearrange("(t r) c -> r t c", t=2))
             elif o == "consts":
-                nc.vector.memset(rows[:], 0.0)
-                nc.scalar.dma_start(out=rows[0:2, :].bitcast(BF16), in_=amp.rearrange("(g c) -> g c", g=2))
-                nc.scalar.dma_start(out=rows[2:4, :].bitcast(BF16), in_=state_scale.rearrange("(g c) -> g c", g=2))
+                nc.gpsimd.memset(rows[:], 0.0)
+                nc.sync.dma_start(out=rows[0:2, :].bitcast(BF16), in_=amp.rearrange("(g c) -> g c", g=2))
+                nc.sync.dma_start(out=rows[2:4, :].bitcast(BF16), in_=state_scale.rearrange("(g c) -> g c", g=2))
                 make_identity(nc, ident[:])
                 nc.vector.memset(one[:], 1.0)
                 nc.scalar.activation(out=warm[:], in_=one[:], func=ACT.Ln)
@@ -298,11 +305,11 @@ def tile_inducing_kernel_mean_h3_kernel(tc, x, z, amp, w, mean, state_scale, out
                 nc.scalar.copy(out=ss_sb[:, 0:512], in_=ss_view(0, 512))
             elif o == "ws":
                 g, h, t = a
-                dst = rot(sb, "wsg", ("ws", g, h), [P, 4, 512], BF16)
+                dst = T[("w", g, h)]
                 nc.vector.tensor_scalar(out=dst[:, t, :], in0=T[("w", g, h)][:, t, :], scalar1=sign[:, 4 * g + t : 4 * g + t + 1], scalar2=None, op0=ALU.mult)
             elif o == "wi":
                 dst = rot(sb, a[3] if len(a) > 3 else "wil", ("wi",) + a[:2], [P, 2048], BF16)
-                interleave(a[2], dst[:], T[("ws",) + a[:2]][:])
+                interleave(a[2], dst[:], T[("w",) + a[:2]][:])
             elif o == "wq":
                 cols = slice(512 * a[1], 512 * a[1] + 512)
                 nc.vector.quantize_mx(out=w_codes[:, a[0], cols].bitcast(FP8X4), scales=w_scales[:, a[0], cols], in_=T[("wi",) + a][:])

@@ -18,10 +18,10 @@ ACT = mybir.ActivationFunctionType
 
 BUFS = dict(sbank=4, s2bank=3, kzi=1, kzv=3, ez=3, y=5, tmp=2, yc=3, yi=3, wsg=4, wil=2, xi=2, zi=2)
 FOUR = "VS"
-GM = dict((s, 320) for s in range(9, 15))
+GM = dict([(s, 128) for s in range(1, 5)] + [(s, 384) for s in range(9, 15)] + [(15, 192)])
 GC = dict((s, 64) for s in range(5, 9))
 GK = {9: 128, 10: 128, 11: 128, 12: 128}
-X3, X3Q, SSC = 2, 4, 5
+X3, X3Q, SSC = 2, 4, 0
 YQ = dict([(s, [s - 4]) for s in range(4, 13)] + [(13, [9, 10]), (14, [11]), (15, [12])])
 EX0 = {2: 1, 3: 5}
 
@@ -32,8 +32,9 @@ def schedule(P):
     def add(*op):
         ops.append(op)
 
+    add("load", *P["loads"][0])
     add("consts")
-    for l in P["loads"]:
+    for l in P["loads"][1:]:
         add("load", *l)
     add("vt")
     for op in P["head"]:
@@ -175,7 +176,7 @@ def tile_inducing_kernel_mean_h3_kernel(tc, x, z, amp, w, mean, state_scale, out
             return T[key]
 
         def keep(name, shape, dtype):
-            return sb.tile(shape, dtype, name=name, tag=name, align_bytes=64)
+            return sb.tile(shape, dtype, name=name, tag=name, align_bytes=256 if dtype in (U32, U8) else 64)
 
         ident = keep("ident", [P, P], F32)
         one = keep("one", [P, 1], F32)
@@ -192,7 +193,7 @@ def tile_inducing_kernel_mean_h3_kernel(tc, x, z, amp, w, mean, state_scale, out
         ln_mant = keep("ln_mant", [P, 8], F32)
         ln_amp = keep("ln_amp", [P, 8], F32)
         ss_bf = keep("ss_bf", [P, 8], BF16)
-        ss_sb = keep("ss_sb", [P, N], BF16)
+        ss_sb = keep("ss_sb", [P, 512], BF16)
         z_codes = keep("z_codes", [P, J], U32)
         z_scales = keep("z_scales", [P, J], U8)
         x_codes = keep("x_codes", [P, M], U32)

import math
from contextlib import ExitStack

import concourse.mybir as mybir
from concourse.masks import make_identity

M, D, J, N = 2048, 512, 1024, 1024
FLOPS = 2 * J * M * D + 2 * M * J * N
P = 128
F32 = mybir.dt.float32
BF16 = mybir.dt.bfloat16
I32 = mybir.dt.int32
U32 = mybir.dt.uint32
U8 = mybir.dt.uint8
FP8X4 = mybir.dt.float8_e4m3fn_x4
ALU = mybir.AluOpType
ACT = mybir.ActivationFunctionType

BUFS = dict(sbank=4, s2bank=3, kzi=1, kzv=3, ez=3, y=5, tmp=2, yc=3, yi=3, wsg=4, wil=2, xi=2, zi=2)
FOUR = "VS"
GM = dict([(s, 128) for s in range(1, 5)] + [(s, 384) for s in range(9, 15)] + [(15, 192)])
GC = dict((s, 64) for s in range(5, 9))
GK = {9: 128, 10: 128, 11: 128, 12: 128}
X3, X3Q, SSC = 2, 4, 0
YQ = dict([(s, [s - 4]) for s in range(4, 13)] + [(13, [9, 10]), (14, [11]), (15, [12])])
EX0 = {2: 1, 3: 5}


def schedule(P):
    ops = []

    def add(*op):
        ops.append(op)

    add("load", *P["loads"][0])
    add("consts")
    for l in P["loads"][1:]:
        add("load", *l)
    add("vt")
    for op in P["head"]:
        add(*op)
    S = 16
    for s in range(S):
        for op in P["g"].get(s, []):
            add(*op)
        add("ad", s, 0)
        add("ad", s, 1)
        if GC.get(s, 0):
            add("ca", s - 1, 0, GC[s], "G")
        if GM.get(s, 0):
            add("mu", s, 0, GM[s], "G")
            add("mu", s, GM[s], 512, "V")
        else:
            add("mu", s, 0, 512, "V")
        if s == S - 1:
            add("sty", s, 0)
        add("mu", s, 512, 1024, "V")
        if s == S - 1:
            add("sty", s, 1)
        else:
            add("sty", s)
        if s >= 1:
            add("ca", s - 1, GC.get(s, 0), 256, "S")
        if s >= 2:
            add("yt", s - 2)
        for op in P["xt"].get(s, []):
            add(*op)
        if s >= 2:
            add("yw", s - 2)
        for op in P["xc"].get(s, []):
            add(*op)
        if s + 1 < S:
            add("s2", s + 1, 0)
            add("s2", s + 1, 1)
        for op in P["ex"].get(s, []):
            add("s1", *op)
            add("ex", *op)
        for op in P["sk"].get(s, []):
            add(*op)
        for op in P["vq"].get(s, []):
            add(*op)
        for n in YQ.get(s, []):
            j, g = divmod(n, 2)
            add("yq", 2 * j, 2 * j + 2, g)
            if g == 1 and j % 2 == 1:
                add("stw", 2 * j - 2, 2 * j + 2)
            if g == 1 and j == 5:
                add("sts", 0, 12)
    add("yt", 14)
    add("ca", 15, 0, 128, "S")
    add("yw", 14)
    add("ca", 15, 128, 256, "V")
    add("yq", 12, 14, 1)
    add("yt", 15, 0)
    add("yt", 15, 1)
    add("yq", 14, 15, 0)
    add("yq", 14, 15, 1)
    add("stw", 12, 15)
    add("yw", 15, 0)
    add("yw", 15, 1)
    add("yq", 15, 16, 0)
    add("yq", 15, 16, 1)
    add("stw", 15, 16)
    add("sts", 12, 16)
    return ops


def params():
    P = {}
    P["loads"] = [("z", 0, 0), ("z", 0, 1), ("w", 0, 0), ("x", 0), ("w", 1, 0), ("w", 0, 1), ("z", 1, 0), ("z", 1, 1), ("x", 1), ("w", 1, 1), ("x", 2), ("mean", 0), ("mean", 1), ("x", 3)] + [("mean", i) for i in range(2, 8)]
    H = []
    ws = lambda g, h: [("ws", g, h, t) for t in range(4)]
    H += [("am", 0), ("am", 1), ("am", 3), ("am", 2), ("am", 4), ("zt", 0, 0), ("zc", 0, 0), ("zt", 0, 1), ("zc", 0, 1), ("ln",)]
    for t in range(4):
        H += [("ws", 0, 0, t)] + [("am", 5 + t)] * (t < 3)
    H += [("wi", 0, 0, "V"), ("zq", 0), ("wq", 0, 0)]
    H += [("xt", 0, 0), ("xt", 0, 1), ("xc", 0, 0), ("xc", 0, 1), ("sst",)]
    H += ws(1, 0) + [("am", 8), ("wi", 1, 0, "S"), ("xq", 0)] + ws(0, 1) + [("wi", 0, 1, "V"), ("wq", 1, 0)]
    H += [("zt", 1, 0), ("zt", 1, 1), ("zc", 1, 0), ("zc", 1, 1)]
    for t in range(4):
        H += [("s1", 0, 0, t), ("ex", 0, 0, t)]
    H += [("wq", 0, 1), ("zq", 1)] + ws(1, 1) + [("wi", 1, 1, "V")]
    H += [("xt", 1, 0), ("xt", 1, 1), ("xc", 1, 0), ("xc", 1, 1)]
    for t in range(4):
        H += [("s1", 0, 1, t), ("ex", 0, 1, t)]
    H += [("xt", 2, 0), ("xt", 2, 1), ("xc", 2, 0), ("xc", 2, 1)]
    H += [("ki", 0, 0, 0, 0, 256, "V", "kzv"), ("ki", 0, 0, 1, 0, 256, "V", "kzi"), ("wq", 1, 1), ("kq", 0, 0, 0), ("xq", 1), ("ki", 0, 1, 0, 0, 256, "V", "kzv"), ("kq", 0, 1, 0), ("xq", 2), ("kq", 0, 0, 1)]
    for t in range(4):
        H += [("s1", 1, 0, t), ("ex", 1, 0, t)]
    H += [("s2", 0, 0), ("s1", 1, 1, 0), ("ex", 1, 1, 0), ("s2", 0, 1), ("s1", 1, 1, 1), ("ex", 1, 1, 1)]
    P["head"] = H
    P["g"], P["vq"], P["ex"], P["xt"], P["xc"], P["sk"] = {}, {}, {}, {}, {}, {}
    P["g"][0] = [("ki", 0, 1, 1, 0, 256, "G", "kzi")]
    P["vq"][0] = [("kq", 0, 1, 1)]
    for k in (1, 2, 3):
        for n, (g, hf) in enumerate([(0, 0), (1, 0), (0, 1), (1, 1)]):
            s = 4 * k - 3 + n
            m1 = GK.get(s, 256)
            P["g"].setdefault(s, [])
            if m1 > 0:
                P["g"][s].append(("ki", k, g, hf, 0, m1, "G", "kzi"))
            if m1 < 256:
                P["g"][s].append(("ki", k, g, hf, m1, 256, "S", "kzi"))
            P["vq"].setdefault(s, []).append(("kq", k, g, hf))
    P["ex"][0] = [(1, 1, t) for t in range(2, 4)]
    for k in (2, 3):
        s0 = EX0[k]
        for n in range(4):
            P["ex"].setdefault(s0 + n, []).extend([(k, n // 2, 2 * (n % 2)), (k, n // 2, 2 * (n % 2) + 1)])
    P["sk"][SSC] = [("ssc",)]
    for n in range(2):
        P["xt"][X3 + n] = [("xt", 3, n)]
        P["xc"][X3 + n] = [("xc", 3, n)]
    P["vq"][X3Q].insert(0, ("xq", 3))
    return P


def tile_inducing_kernel_mean_h3_kernel(tc, x, z, amp, w, mean, state_scale, out_0, out_1, out_2):
    nc = tc.nc
    with ExitStack() as ctx:
        sb = ctx.enter_context(tc.tile_pool(name="sb", bufs=1))
        ps = ctx.enter_context(tc.psum_pool(name="ps", bufs=1))
        ctx.enter_context(tc.manual_schedule())
        T = {}
        count = {}

        def rot(pool, tag, key, shape, dtype):
            if key not in T:
                n = count.get(tag, 0)
                count[tag] = n + 1
                name = "%s%d" % (tag, n % BUFS[tag])
                if pool is ps:
                    T[key] = pool.tile(shape, dtype, name=name, tag=name)
                else:
                    T[key] = pool.tile(shape, dtype, name=name, tag=name, align_bytes=64)
            return T[key]

        def keep(name, shape, dtype):
            return sb.tile(shape, dtype, name=name, tag=name, align_bytes=256 if dtype in (U32, U8) else 64)

        ident = keep("ident", [P, P], F32)
        one = keep("one", [P, 1], F32)
        warm = keep("warm", [P, 1], F32)
        rows = keep("rows", [P, 256], F32)
        amp_bf = keep("amp_bf", [P, 8], BF16)
        mant = keep("mant", [P, 4], I32)
        exp_i = keep("exp_i", [P, 8], I32)
        exp_f = keep("exp_f", [P, 8], F32)
        sign2 = keep("sign2", [P, 8], F32)
        sign = keep("sign", [P, 8], F32)
        dead = keep("dead", [P, 8], F32)
        ln_part = keep("ln_part", [P, 8], F32)
        ln_mant = keep("ln_mant", [P, 8], F32)
        ln_amp = keep("ln_amp", [P, 8], F32)
        ss_bf = keep("ss_bf", [P, 8], BF16)
        ss_sb = keep("ss_sb", [P, 512], BF16)
        z_codes = keep("z_codes", [P, J], U32)
        z_scales = keep("z_scales", [P, J], U8)
        x_codes = keep("x_codes", [P, M], U32)
        x_scales = keep("x_scales", [P, M], U8)
        w_codes = keep("w_codes", [P, 2, N], U32)
        w_scales = keep("w_scales", [P, 2, N], U8)
        k_codes = keep("k_codes", [P, 2, M], U32)
        k_scales = keep("k_scales", [P, 2, M], U8)
        y_codes = keep("y_codes", [P, 2, M], U32)
        y_scales = keep("y_scales", [P, 2, M], U8)
        ss_bank = ps.tile([P, 512], F32, name="ss_bank", tag="ss_bank")
        words_out = out_1.rearrange("g p m t -> p g (m t)").bitcast(I32)

        def interleave(eng, dst, src):
            if eng in FOUR:
                d = dst.rearrange("p (c i t) -> p c t i", i=4, t=4)
                s = src.rearrange("p t (c i) -> p c t i", i=4)
            else:
                d = dst.rearrange("p (c t) -> p c t", t=4)
                s = src.rearrange("p t c -> p c t")
            if eng == "V":
                nc.vector.tensor_copy(out=d, in_=s)
            elif eng == "S":
                nc.scalar.copy(out=d, in_=s)
            else:
                nc.gpsimd.tensor_scalar(out=d, in0=s, scalar1=1.0, scalar2=1.0, op0=ALU.mult, op1=ALU.mult)

        def ss_view(c0, c1):
            return ss_bank[:].bitcast(BF16)[:, c0:c1]

        for op in schedule(params()):
            o, a = op[0], op[1:]
            if o == "load":
                if a[0] == "z":
                    if ("z", a[1]) not in T:
                        T[("z", a[1])] = keep("z%d" % a[1], [P, 4, D], BF16)
                    ts = slice(2 * a[2], 2 * a[2] + 2)
                    nc.sync.dma_start(out=T[("z", a[1])][:, ts, :], in_=z[512 * a[1] : 512 * a[1] + 512, :].rearrange("(r t) d -> r t d", t=4)[:, ts, :])
                elif a[0] == "x":
                    T[a] = keep("x%d" % a[1], [P, 4, D], BF16)
                    nc.sync.dma_start(out=T[a][:].rearrange("r (a e) d -> r a e d", e=2), in_=x[512 * a[1] : 512 * a[1] + 512, :].rearrange("(a r e) d -> r a e d", a=2, e=2))
                elif a[0] == "w":
                    T[a] = keep("w%d%d" % a[1:], [P, 4, 512], BF16)
                    nc.sync.dma_start(out=T[a][:], in_=w[512 * a[1] : 512 * a[1] + 512, 512 * a[2] : 512 * a[2] + 512].rearrange("(p t) c -> p t c", t=4))
                else:
                    T[a] = keep("mean%d" % a[1], [P, 2, N], BF16)
                    nc.sync.dma_start(out=T[a][:], in_=mean[256 * a[1] : 256 * a[1] + 256, :].rearrange("(t r) c -> r t c", t=2))
            elif o == "consts":
                nc.gpsimd.memset(rows[:], 0.0)
                nc.sync.dma_start(out=rows[0:2, :].bitcast(BF16), in_=amp.rearrange("(g c) -> g c", g=2))
                nc.sync.dma_start(out=rows[2:4, :].bitcast(BF16), in_=state_scale.rearrange("(g c) -> g c", g=2))
                make_identity(nc, ident[:])
                nc.vector.memset(one[:], 1.0)
                nc.scalar.activation(out=warm[:], in_=one[:], func=ACT.Ln)
            elif o == "vt":
                bank = rot(ps, "sbank", op, [P, 512], F32)
                for u in range(2):
                    nc.tensor.transpose(bank[:, 128 * u : 128 * u + 128], rows[:, u:256:2], ident[:])
                for u in range(2):
                    nc.tensor.transpose(bank[:, 256 + 128 * u : 384 + 128 * u], rows[:, 128 * u : 128 * u + 128], ident[:])
                view = bank[:].rearrange("p (k r) -> p r k", k=4)
                nc.vector.tensor_copy(out=amp_bf[:].bitcast(F32).rearrange("p (g u) -> p g u", g=2), in_=view[:, 0:2, 0:2])
                nc.vector.tensor_copy(out=ss_bf[:].bitcast(F32).rearrange("p (g u) -> p g u", g=2), in_=view[:, 2:4, 2:4])
            elif o == "am":
                words = amp_bf[:].bitcast(I32)
                if a[0] == 0:
                    nc.vector.tensor_scalar(out=sign2[:], in0=amp_bf[:], scalar1=0.0, scalar2=2.0, op0=ALU.is_ge, op1=ALU.mult)
                elif a[0] == 1:
                    nc.vector.tensor_scalar(out=mant[:], in0=words, scalar1=0x007F007F, scalar2=0x3F803F80, op0=ALU.bitwise_and, op1=ALU.bitwise_or)
                elif a[0] == 2:
                    nc.vector.tensor_scalar(out=sign[:], in0=sign2[:], scalar1=-1.0, scalar2=None, op0=ALU.add)
                elif a[0] in (3, 4):
                    e = a[0] - 3
                    nc.vector.tensor_scalar(out=exp_i[:, e:8:2], in0=words, scalar1=7 + 16 * e, scalar2=255, op0=ALU.logical_shift_right, op1=ALU.bitwise_and)
                elif a[0] == 5:
                    nc.vector.tensor_copy(out=exp_f[:], in_=exp_i[:])
                elif a[0] == 6:
                    nc.vector.tensor_scalar(out=dead[:], in0=exp_f[:], scalar1=0.0, scalar2=-4096.0, op0=ALU.is_equal, op1=ALU.mult)
                elif a[0] == 7:
                    nc.vector.scalar_tensor_tensor(out=ln_part[:], in0=exp_f[:], scalar=-127.0, in1=dead[:], op0=ALU.add, op1=ALU.add)
                else:
                    nc.vector.scalar_tensor_tensor(out=ln_amp[:], in0=ln_part[:], scalar=math.log(2.0), in1=ln_mant[:], op0=ALU.mult, op1=ALU.add)
            elif o == "ln":
                nc.scalar.activation(out=ln_mant[:], in_=mant[:].bitcast(BF16), func=ACT.Ln)
                nc.scalar.activation(out=warm[:], in_=one[:], func=ACT.Exp)
            elif o in ("zt", "xt"):
                bank = rot(ps, "sbank", op, [P, 512], F32)
                for r in range(2):
                    words = T[(o[0], a[0])][:, 2 * a[1] + r, :].bitcast(F32)
                    for u in range(2):
                        c0 = 256 * r + 128 * u
                        nc.tensor.transpose(bank[:, c0 : c0 + 128], words[:, u:256:2], ident[:])
            elif o in ("zc", "xc"):
                dst = rot(sb, o[0] + "i", (o[0] + "i", a[0]), [P, 2048], BF16)
                bank = T[(o[0] + "t",) + a]
                words = dst[:, 1024 * a[1] : 1024 * a[1] + 1024].bitcast(F32)
                if o == "zc":
                    nc.scalar.copy(out=words.rearrange("p (r m u) -> p r m u", r=2, u=2), in_=bank[:].rearrange("p (r u m) -> p r m u", r=2, u=2))
                else:
                    nc.scalar.copy(out=words.rearrange("p (m k) -> p m k", k=4), in_=bank[:].rearrange("p (k m) -> p m k", k=4))
            elif o in ("zq", "xq"):
                codes, scales = (z_codes, z_scales) if o == "zq" else (x_codes, x_scales)
                cols = slice(512 * a[0], 512 * a[0] + 512)
                nc.vector.quantize_mx(out=codes[:, cols].bitcast(FP8X4), scales=scales[:, cols], in_=T[(o[0] + "i", a[0])][:])
            elif o == "sst":
                words = ss_bf[:].bitcast(F32)
                for i in range(4):
                    nc.tensor.transpose(ss_bank[:, 128 * i : 128 * i + 128], words[:, i : i + 1].to_broadcast([P, P]), ident[:])
            elif o == "ssc":
                nc.scalar.copy(out=ss_sb[:, 0:512], in_=ss_view(0, 512))
            elif o == "ws":
                g, h, t = a
                dst = T[("w", g, h)]
                nc.vector.tensor_scalar(out=dst[:, t, :], in0=T[("w", g, h)][:, t, :], scalar1=sign[:, 4 * g + t : 4 * g + t + 1], scalar2=None, op0=ALU.mult)
            elif o == "wi":
                dst = rot(sb, a[3] if len(a) > 3 else "wil", ("wi",) + a[:2], [P, 2048], BF16)
                interleave(a[2], dst[:], T[("w",) + a[:2]][:])
            elif o == "wq":
                cols = slice(512 * a[1], 512 * a[1] + 512)
                nc.vector.quantize_mx(out=w_codes[:, a[0], cols].bitcast(FP8X4), scales=w_scales[:, a[0], cols], in_=T[("wi",) + a][:])
            elif o == "s1":
                k, g, t = a
                bank = rot(ps, "sbank", op, [P, 512], F32)
                jc = slice(512 * g + 128 * t, 512 * g + 128 * t + 128)
                mc = slice(512 * k, 512 * k + 512)
                nc.tensor.matmul_mx(out=bank[:], lhsT=z_codes[:, jc].bitcast(FP8X4), lhsT_scale=z_scales[:, jc], rhs=x_codes[:, mc].bitcast(FP8X4), rhs_scale=x_scales[:, mc], start=True, stop=True)
            elif o == "ex":
                k, g, t = a
                dst = rot(sb, "ez", ("ez", k, g), [P, 4, 512], BF16)
                col = 4 * g + t
                nc.scalar.activation(out=dst[:, t, :], in_=T[("s1",) + a][:], func=ACT.Exp, bias=ln_amp[:, col : col + 1])
            elif o == "ki":
                k, g, hf, m0, m1, eng, tag = a
                dst = rot(sb, tag, ("ki", k, g, hf), [P, 1024], BF16)
                interleave(eng, dst[:, 4 * m0 : 4 * m1], T[("ez", k, g)][:, :, 256 * hf + m0 : 256 * hf + m1])
            elif o == "kq":
                k, g, hf = a
                cols = slice(512 * k + 256 * hf, 512 * k + 256 * hf + 256)
                nc.vector.quantize_mx(out=k_codes[:, g, cols].bitcast(FP8X4), scales=k_scales[:, g, cols], in_=T[("ki",) + a][:])
            elif o == "s2":
                i, h = a
                bank = rot(ps, "s2bank", op, [P, 512], F32)
                mc = slice(128 * i, 128 * i + 128)
                cc = slice(512 * h, 512 * h + 512)
                for g in range(2):
                    nc.tensor.matmul_mx(out=bank[:], lhsT=k_codes[:, g, mc].bitcast(FP8X4), lhsT_scale=k_scales[:, g, mc], rhs=w_codes[:, g, cc].bitcast(FP8X4), rhs_scale=w_scales[:, g, cc], start=(g == 0), stop=(g == 1))
            elif o == "ad":
                i, h = a
                dst = rot(sb, "tmp", ("tmp", i), [P, N], F32)
                cc = slice(512 * h, 512 * h + 512)
                nc.vector.tensor_tensor(out=dst[:, cc], in0=T[("s2", i, h)][:], in1=T[("mean", i // 2)][:, i % 2, cc], op=ALU.add)
            elif o == "mu":
                i, c0, c1, eng = a
                dst = rot(sb, "y", ("y", i), [P, N], F32)
                cc = slice(c0, c1)
                if eng == "G":
                    nc.gpsimd.tensor_tensor(out=dst[:, cc], in0=T[("tmp", i)][:, cc], in1=ss_sb[:, cc], op=ALU.mult)
                else:
                    nc.vector.tensor_tensor(out=dst[:, cc], in0=T[("tmp", i)][:, cc], in1=ss_view(c0, c1), op=ALU.mult)
            elif o == "sty":
                i = a[0]
                cc = slice(0, N) if len(a) == 1 else slice(512 * a[1], 512 * a[1] + 512)
                nc.sync.dma_start(out=out_0[128 * i : 128 * i + 128, cc], in_=T[("y", i)][:, cc])
            elif o == "ca":
                i, q0, q1, eng = a
                dst = rot(sb, "yc", ("yc", i), [P, N], BF16)
                d = dst[:].rearrange("m (u q e) -> m u q e", u=2, e=2)[:, :, q0:q1, :]
                s = T[("y", i)][:].rearrange("m (q u e) -> m u q e", u=2, e=2)[:, :, q0:q1, :]
                if eng == "V":
                    nc.vector.tensor_copy(out=d, in_=s)
                elif eng == "S":
                    nc.scalar.copy(out=d, in_=s)
                else:
                    nc.gpsimd.tensor_scalar(out=d, in0=s, scalar1=1.0, scalar2=1.0, op0=ALU.mult, op1=ALU.mult)
            elif o == "yt":
                i = a[0]
                bank = rot(ps, "sbank", op, [P, 512], F32)
                words = T[("yc", i)][:].bitcast(F32)
                for g in (range(2) if len(a) == 1 else [a[1]]):
                    for u in range(2):
                        c0, w0 = 256 * g + 128 * u, 256 * u + 128 * g
                        nc.tensor.transpose(bank[:, c0 : c0 + 128], words[:, w0 : w0 + 128], ident[:])
            elif o == "yw":
                i = a[0]
                dst = rot(sb, "yi", ("yi", i // 2), [P, 2, 1024], BF16)
                gs = slice(0, 2) if len(a) == 1 else slice(a[1], a[1] + 1)
                nc.scalar.copy(
                    out=dst[:, gs, 512 * (i % 2) : 512 * (i % 2) + 512].bitcast(F32).rearrange("p g (m u) -> p g m u", u=2),
                    in_=T[("yt",) + a][:].rearrange("p (g u m) -> p g m u", g=2, u=2)[:, gs],
                )
            elif o == "yq":
                i0, i1, g = a
                mc = slice(128 * i0, 128 * i1)
                nc.vector.quantize_mx(out=y_codes[:, g, mc].bitcast(FP8X4), scales=y_scales[:, g, mc], in_=T[("yi", i0 // 2)][:, g, 512 * (i0 % 2) : 512 * (i0 % 2) + 512 * (i1 - i0)])
            elif o == "stw":
                mc = slice(128 * a[0], 128 * a[1])
                nc.sync.dma_start(out=words_out[:, :, mc], in_=y_codes[:, :, mc].bitcast(I32))
            elif o == "sts":
                mc = slice(128 * a[0], 128 * a[1])
                for q in range(4):
                    eng = nc.scalar if (a[1] == 16 and q >= 2) else nc.sync
                    eng.dma_start(
                        out=out_2[:, 4 * q : 4 * q + 4, mc].rearrange("g r m -> r g m").bitcast(I32),
                        in_=y_scales[32 * q : 32 * q + 4, :, mc].bitcast(I32),
                    )
            else:
                raise ValueError(o)
